import numpy as np
import ml_dtypes


def mxq(x, axis, fmt="e4m3"):
    dtype, down = {"e4m3": (ml_dtypes.float8_e4m3fn, 7), "e5m2": (ml_dtypes.float8_e5m2, 14)}[fmt]
    v = np.moveaxis(np.asarray(x, np.float32).astype(ml_dtypes.bfloat16).astype(np.float64), axis, -1)
    blocks = v.reshape(v.shape[:-1] + (-1, 32))
    amax = np.abs(blocks).max(-1, keepdims=True)
    byte = np.maximum(np.where(amax > 0, np.frexp(amax)[1] - 1 + 127, 0) - down, 1)
    scale = np.exp2(byte - 127.0)
    codes = (blocks / scale).astype(np.float32).astype(dtype).astype(np.float64)
    return np.moveaxis((codes * scale).reshape(v.shape), -1, axis)


WIDE = False


def mx_kscale(k):
    if not WIDE:
        return np.ones(k)
    levels = np.array([10, -10, 5, -5, 0])
    if k % 512:
        return np.exp2(np.random.permutation(np.resize(levels, k // 32))).repeat(32)
    a = np.empty((k // 512, 16))
    for p in range(k // 512):
        a[p, :8] = np.random.permutation(np.resize(levels, 8))
        for g in range(8):
            far = levels[np.abs(levels - a[p, g]) >= 10]
            a[p, g + 8] = far[np.random.randint(len(far))]
    return np.exp2(a.ravel()).repeat(32)


def f64(x):
    return np.asarray(x).astype(np.float64)


def striped(idx):
    return np.tile(idx.reshape(-1, 16).T, (8, 1)).astype(np.uint16)


def unstriped(offs):
    return offs[:16].T.reshape(-1).astype(np.int64)


def striped8(idx):
    return np.concatenate([x.reshape(-1, 16).T for x in idx]).astype(np.uint16)


def runs(offs, k):
    lists = np.stack([offs[16 * r : 16 * r + 16].T.reshape(-1) for r in range(8)]).astype(np.int64)
    return lists[np.arange(k) % 512 // 64]


def pack_weight(w):
    k, n = w.shape
    w = f64(np.asarray(w, np.float32).astype(ml_dtypes.bfloat16)).reshape(k // 32, 32, n)
    amax = np.abs(w).max(1)
    byte = np.clip(np.where(amax > 0, np.frexp(amax)[1] - 1 + 127 - 7, 1), 1, 254)
    scaled = (w * np.exp2(127.0 - byte)[:, None, :]).reshape(k, n).astype(np.float32)
    words = np.ascontiguousarray(scaled.reshape(k // 512, 128, 4, n).transpose(0, 1, 3, 2)).astype(ml_dtypes.float8_e4m3fn).view(np.uint8)
    return words, np.ascontiguousarray(byte.astype(np.uint8).reshape(k // 512, 16, n))


def unpack_weight(words, scales):
    g, p, n, _ = words.shape
    vals = np.ascontiguousarray(words).view(ml_dtypes.float8_e4m3fn).astype(np.float64) * np.repeat(np.exp2(scales.astype(np.float64) - 127.0), 8, axis=1)[..., None]
    return vals.transpose(0, 1, 3, 2).reshape(g * 512, n)


def sigmoid(v):
    return 1.0 / (1.0 + np.exp(-np.maximum(v, -700.0)))

def planes(y):
    n, m = y.shape
    v = y.astype(np.float32).astype(ml_dtypes.bfloat16).astype(np.float64).reshape(n // 32, 32, m)
    top = np.abs(v).max(1)
    byte = np.clip(np.where(top > 0, np.frexp(top)[1] - 1 + 127 - 7, 1), 1, 254)
    codes = (v * np.exp2(127.0 - byte)[:, None, :]).reshape(n, m).astype(np.float32).astype(ml_dtypes.float8_e4m3fn).view(np.uint8)
    words = codes.reshape(n // 512, 128, 4, m).transpose(0, 1, 3, 2)
    return np.ascontiguousarray(words), np.ascontiguousarray(byte.astype(np.uint8).reshape(n // 512, 16, m))


K, T, S, G, H, C = 512, 1024, 256, 2048, 512, 512


def setup_inputs():
    n = np.random.standard_normal
    s = mx_kscale(K)[:, None]
    packed_xT = pack_weight(n((K, T)) * s)
    packed_dT = pack_weight(n((K, G)) / s)
    return {
        "x_words": packed_xT[0],
        "x_scales": packed_xT[1],
        "d_words": packed_dT[0],
        "d_scales": packed_dT[1],
        "tau": np.random.uniform(0.3, 0.9, (H, 1)).astype(np.float32),
        "gs": (np.random.uniform(0.5, 1.5, (K, 1)) / s).astype(np.float32),
        "sl": np.random.uniform(1.0, 2.0, (H, 1)).astype(np.float32),
        "th": (0.5 * n((H, 1))).astype(np.float32),
        "offs": striped(np.random.permutation(T)[:S]),
        "k1": striped8(np.random.randint(0, G, (8, H))),
        "n1": striped(np.random.permutation(S)),
        "n2": striped(np.random.permutation(S)),
        "cand": striped(np.random.permutation(T)[:C]),
        "two": striped(np.random.permutation(T)[:S]),
        "k2": striped8(np.random.randint(0, G, (8, H))),
        "n3": striped(np.random.permutation(S)),
        "n4": striped(np.random.permutation(S)),
    }


def reference(x_words, x_scales, d_words, d_scales, tau, gs, sl, th, offs, k1, n1, n2, cand, two, k2, n3, n4):
    x_cand = unpack_weight(x_words, x_scales)[:, unstriped(cand)]
    d_k1 = unpack_weight(d_words, d_scales)[np.arange(K)[:, None], runs(k1, K)]
    xq = unpack_weight(x_words, x_scales)[:, unstriped(offs)]
    h = 0.0625 * (d_k1.T @ xq)
    low = h.min(axis=1, keepdims=True)
    ea = np.exp(f64(tau) * (low - h[:, unstriped(n1)]))
    z = f64(gs) * (h - (2.0 * (ea * h[:, unstriped(n2)])))
    a = 0.0625 * ((x_cand.T @ mxq(z, 0, "e4m3")))
    d_k2 = unpack_weight(d_words, d_scales)[np.arange(K)[:, None], runs(k2, K)]
    x_two = unpack_weight(x_words, x_scales)[:, unstriped(two)]
    b = 0.0625 * (d_k2.T @ x_two)
    sg = sigmoid(f64(sl) * (b[:, unstriped(n3)] - f64(th)))
    out_0 = a * sg - (0.5 * a[:, unstriped(n4)])
    return (out_0,) + planes(out_0)

@@ -1,0 +1,205 @@
+from contextlib import ExitStack
+
+import concourse.mybir as mybir
+
+K, T, S, G, H, C = 512, 1024, 256, 2048, 512, 512
+FLOPS = 3 * 2 * K * H * S
+
+F32 = mybir.dt.float32
+BF16 = mybir.dt.bfloat16
+I32 = mybir.dt.int32
+U32 = mybir.dt.uint32
+U16 = mybir.dt.uint16
+U8 = mybir.dt.uint8
+FP8X4 = mybir.dt.float8_e4m3fn_x4
+ALU = mybir.AluOpType
+ACT = mybir.ActivationFunctionType
+
+P = 128
+PACK = 4
+SIXTEENTH = 0.0625
+
+
+def tile_picked_pqcjgxbebz_none_po_kernel(
+    tc, x_words, x_scales, d_words, d_scales, tau, gs, sl, th, offs, k1, n1, n2, cand, two, k2, n3, n4, out_0, out_1, out_2
+):
+    nc = tc.nc
+    with ExitStack() as ctx:
+        held = ctx.enter_context(tc.tile_pool(name="held", bufs=1))
+        psum = ctx.enter_context(tc.psum_pool(name="psum", bufs=1))
+
+        def load_list(name, src):
+            tile = held.tile(list(src.shape), U16, name=name)
+            nc.sync.dma_start(tile[:], src)
+            return tile
+
+        def load_scale_rows(name, src, width):
+            tile = held.tile([P, width], U8, name=name, align_bytes=64)
+            rows = src[0].bitcast(I32).unsqueeze(1).to_broadcast([16, 8, width // 4])
+            nc.sync.dma_start(tile[:].bitcast(I32), rows)
+            return tile
+
+        def load_words(name, src, width):
+            tile = held.tile([P, width], U32, name=name, align_bytes=64)
+            nc.sync.dma_start(tile[:].bitcast(I32), src[0].rearrange("p n t -> p (n t)").bitcast(I32))
+            return tile
+
+        def load_rows(name, src):
+            tile = held.tile([P, PACK], F32, name=name)
+            nc.gpsimd.dma_start(tile[:], src.rearrange("(p t) o -> p (t o)", t=PACK))
+            return tile
+
+        k1_t = load_list("k1_t", k1)
+        d_bytes = load_scale_rows("d_bytes", d_scales, G)
+        offs_t = load_list("offs_t", offs)
+        x_bytes = load_scale_rows("x_bytes", x_scales, T)
+        d_tab = load_words("d_tab", d_words, G)
+        x_tab = load_words("x_tab", x_words, T)
+        k2_t = load_list("k2_t", k2)
+        n1_t = load_list("n1_t", n1)
+        n2_t = load_list("n2_t", n2)
+        two_t = load_list("two_t", two)
+        cand_t = load_list("cand_t", cand)
+        n3_t = load_list("n3_t", n3)
+        n4_t = load_list("n4_t", n4)
+        tau_t = load_rows("tau_t", tau)
+        gs_t = load_rows("gs_t", gs)
+        sl_t = load_rows("sl_t", sl)
+        th_t = load_rows("th_t", th)
+
+        neg_tau = held.tile([P, PACK], F32, name="neg_tau")
+        nc.gpsimd.tensor_scalar(neg_tau[:], tau_t[:], -1.0, 0.0, ALU.mult, ALU.add)
+        gs_m2 = held.tile([P, PACK], F32, name="gs_m2")
+        nc.gpsimd.tensor_scalar(gs_m2[:], gs_t[:], -2.0, 0.0, ALU.mult, ALU.add)
+        gs_16 = held.tile([P, PACK], F32, name="gs_16")
+        nc.gpsimd.tensor_scalar(gs_16[:], gs_t[:], SIXTEENTH, 0.0, ALU.mult, ALU.add)
+        sl_th = held.tile([P, PACK], F32, name="sl_th")
+        nc.gpsimd.tensor_tensor(sl_th[:], sl_t[:], th_t[:], ALU.mult)
+        sg_bias = held.tile([P, PACK], F32, name="sg_bias")
+        nc.gpsimd.tensor_scalar(sg_bias[:], sl_th[:], -1.0, 0.0, ALU.mult, ALU.add)
+
+        h_win = [held.tile([P, 2 * S], F32, name="h_win%d" % t) for t in range(PACK)]
+        b_win = [held.tile([P, 2 * S], F32, name="b_win%d" % t) for t in range(PACK)]
+        a_win = [held.tile([P, 2 * S], F32, name="a_win%d" % t) for t in range(PACK)]
+        for t in range(PACK):
+            nc.vector.memset(h_win[t][:, S:], 0.0)
+
+        def deal_words(dst, src):
+            nc.vector.tensor_copy(
+                dst[:].bitcast(I32).rearrange("p (t c i) -> p c t i", t=PACK, i=4),
+                src[:].bitcast(I32).rearrange("p (c i t) -> p c t i", t=PACK, i=4),
+            )
+
+        def deal_bytes(dst, src):
+            nc.vector.tensor_copy(dst.rearrange("p (t m) -> p t m", t=PACK), src.rearrange("p (m t) -> p t m", t=PACK))
+
+        def place_scale_rows(plane):
+            words = plane[:].bitcast(I32)
+            for r in range(1, 4):
+                nc.sync.dma_start(words[r:P:32, :], words[8 * r : P : 32, :])
+
+        def product(banks, lhs_words, lhs_scales, rhs_words, rhs_scales):
+            for t in range(PACK):
+                cols = slice(t * P, (t + 1) * P)
+                nc.tensor.matmul_mx(
+                    out=banks[t][:, :S],
+                    lhsT=lhs_words[:, cols].bitcast(FP8X4),
+                    lhsT_scale=lhs_scales[:, cols],
+                    rhs=rhs_words.bitcast(FP8X4),
+                    rhs_scale=rhs_scales,
+                    start=True,
+                    stop=True,
+                )
+
+        got_b1 = held.tile([P, H + S], U8, name="got_b1", align_bytes=64)
+        nc.vector.tensor_copy(got_b1[:, :H], d_bytes[:].indirect(k1_t[:]))
+        nc.vector.tensor_copy(got_b1[:, H:], x_bytes[:].indirect(offs_t[:]))
+        plane1 = held.tile([P, H + S], U8, name="plane1", tag="bytes_a", align_bytes=64)
+        deal_bytes(plane1[:, :H], got_b1[:, :H])
+        nc.vector.tensor_copy(plane1[:, H:].bitcast(I32), got_b1[:, H:].bitcast(I32))
+        place_scale_rows(plane1)
+        got_k1 = held.tile([P, H], U32, name="got_k1", tag="words_a", align_bytes=64)
+        nc.vector.tensor_copy(got_k1[:], d_tab[:].indirect(k1_t[:]))
+        k1_w = held.tile([P, H], U32, name="k1_w", tag="words_b", align_bytes=64)
+        deal_words(k1_w, got_k1)
+        offs_w = held.tile([P, S], U32, name="offs_w", tag="words_c", align_bytes=64)
+        nc.vector.tensor_copy(offs_w[:], x_tab[:].indirect(offs_t[:]))
+        h_ps = [psum.tile([P, 2 * S], F32, name="h_ps%d" % t, tag="ha%d" % t) for t in range(PACK)]
+        product(h_ps, k1_w, plane1, offs_w[:], plane1[:, H:])
+
+        low = held.tile([P, PACK], F32, name="low")
+        ea_bias = held.tile([P, PACK], F32, name="ea_bias")
+        h_n2 = held.tile([P, PACK, S], F32, name="h_n2")
+        gs_h = held.tile([P, PACK, S], F32, name="gs_h")
+        for t in range(PACK):
+            col = slice(t, t + 1)
+            nc.vector.tensor_scalar(h_win[t][:, :S], h_ps[t][:, :S], SIXTEENTH, None, ALU.mult, ALU.min, accum_out=low[:, col])
+            nc.gpsimd.tensor_tensor(ea_bias[:, col], tau_t[:, col], low[:, col], ALU.mult)
+            nc.scalar.activation(b_win[t][:, S:], h_win[t][:].indirect(n1_t[:]), ACT.Exp, bias=ea_bias[:, col], scale=neg_tau[:, col])
+        for t in range(PACK):
+            nc.scalar.activation(h_n2[:, t, :], h_win[t][:].indirect(n2_t[:]), ACT.Copy)
+            nc.scalar.activation(gs_h[:, t, :], h_ps[t][:, :S], ACT.Copy, scale=gs_16[:, t : t + 1])
+
+        plane2 = held.tile([P, H + C + S], U8, name="plane2", align_bytes=64)
+        got_b2 = held.tile([P, H], U8, name="got_b2", align_bytes=64)
+        nc.vector.tensor_copy(got_b2[:], d_bytes[:].indirect(k2_t[:]))
+        deal_bytes(plane2[:, :H], got_b2[:])
+        got_b3 = held.tile([P, C + S], U8, name="got_b3", tag="bytes_a", align_bytes=64)
+        nc.vector.tensor_copy(got_b3[:, C:], x_bytes[:].indirect(two_t[:]))
+        nc.vector.tensor_copy(got_b3[:, :C], x_bytes[:].indirect(cand_t[:]))
+        deal_bytes(plane2[:, H : H + C], got_b3[:, :C])
+        nc.vector.tensor_copy(plane2[:, H + C :].bitcast(I32), got_b3[:, C:].bitcast(I32))
+        place_scale_rows(plane2)
+        got_k2 = held.tile([P, H], U32, name="got_k2", tag="words_b", align_bytes=64)
+        nc.vector.tensor_copy(got_k2[:], d_tab[:].indirect(k2_t[:]))
+        k2_w = held.tile([P, H], U32, name="k2_w", tag="words_a", align_bytes=64)
+        deal_words(k2_w, got_k2)
+        two_w = held.tile([P, S], U32, name="two_w", tag="words_c", align_bytes=64)
+        nc.vector.tensor_copy(two_w[:], x_tab[:].indirect(two_t[:]))
+        b_ps = [psum.tile([P, 2 * S], F32, name="b_ps%d" % t) for t in range(PACK)]
+        product(b_ps, k2_w, plane2, two_w[:], plane2[:, H + C :])
+        for t in range(PACK):
+            nc.scalar.activation(b_win[t][:, :S], b_ps[t][:, :S], ACT.Copy, scale=SIXTEENTH)
+        for t in range(PACK):
+            col = slice(t, t + 1)
+            nc.scalar.activation(a_win[t][:, S:], b_win[t][:].indirect(n3_t[:]), ACT.Sigmoid, bias=sg_bias[:, col], scale=sl_t[:, col])
+
+        got_cand = held.tile([P, C], U32, name="got_cand", tag="words_b", align_bytes=64)
+        nc.vector.tensor_copy(got_cand[:], x_tab[:].indirect(cand_t[:]))
+        cand_w = held.tile([P, C], U32, name="cand_w", align_bytes=64)
+        deal_words(cand_w, got_cand)
+        pull = held.tile([P, PACK, S], F32, name="pull")
+        for t in range(PACK):
+            nc.vector.scalar_tensor_tensor(pull[:, t, :], b_win[t][:, S:], gs_m2[:, t : t + 1], h_n2[:, t, :], ALU.mult, ALU.mult)
+        z_bf = held.tile([P, S * PACK], BF16, name="z_bf", align_bytes=64)
+        nc.vector.tensor_tensor(
+            z_bf[:].rearrange("p (c i t) -> p c t i", i=4, t=PACK),
+            gs_h[:].rearrange("p t (c i) -> p c t i", i=4),
+            pull[:].rearrange("p t (c i) -> p c t i", i=4),
+            ALU.add,
+        )
+        z_w = held.tile([P, S], U32, name="z_w", align_bytes=64)
+        z_s = held.tile([P, S], U8, name="z_s", align_bytes=64)
+        nc.vector.quantize_mx(out=z_w[:].bitcast(FP8X4), scales=z_s[:], in_=z_bf[:])
+        a_ps = [psum.tile([P, 2 * S], F32, name="a_ps%d" % t, tag="ha%d" % t) for t in range(PACK)]
+        product(a_ps, cand_w, plane2[:, H : H + C], z_w[:], z_s[:])
+
+        a_n4 = held.tile([P, PACK, S], F32, name="a_n4")
+        gated = held.tile([P, PACK, S], F32, name="gated")
+        y = held.tile([P, PACK, S], F32, name="y")
+        out_rows = out_0.rearrange("(p t) j -> p t j", t=PACK)
+        for t in range(PACK):
+            nc.scalar.activation(a_win[t][:, :S], a_ps[t][:, :S], ACT.Copy, scale=-0.5 * SIXTEENTH)
+            nc.scalar.activation(a_n4[:, t, :], a_win[t][:].indirect(n4_t[:]), ACT.Copy)
+            nc.vector.scalar_tensor_tensor(gated[:, t, :], a_win[t][:, :S], -2.0, a_win[t][:, S:], ALU.mult, ALU.mult)
+            nc.vector.tensor_tensor(y[:, t, :], gated[:, t, :], a_n4[:, t, :], ALU.add)
+            nc.sync.dma_start(out_rows[:, t, :], y[:, t, :])
+        y_bf = held.tile([P, S * PACK], BF16, name="y_bf", align_bytes=64)
+        nc.vector.tensor_copy(y_bf[:].rearrange("p (c i t) -> p c t i", i=4, t=PACK), y[:].rearrange("p t (c i) -> p c t i", i=4))
+        y_w = held.tile([P, S], U32, name="y_w", align_bytes=64)
+        y_s = held.tile([P, S], U8, name="y_s", align_bytes=64)
+        nc.vector.quantize_mx(out=y_w[:].bitcast(FP8X4), scales=y_s[:], in_=y_bf[:])
+        nc.sync.dma_start(out_1[0].rearrange("p c r -> p (c r)").bitcast(I32), y_w[:].bitcast(I32))
+        for r in range(4):
+            queue = nc.scalar if r % 2 else nc.sync
+            queue.dma_start(out_2[0].bitcast(I32)[r:16:4, :], y_s[:].bitcast(I32)[r:P:32, :])

@@ -56,9 +56,9 @@ def tile_picked_pqcjgxbebz_none_po_kernel(
         d_tab = load_words("d_tab", d_words, G)
         x_tab = load_words("x_tab", x_words, T)
         k2_t = load_list("k2_t", k2)
+        two_t = load_list("two_t", two)
         n1_t = load_list("n1_t", n1)
         n2_t = load_list("n2_t", n2)
-        two_t = load_list("two_t", two)
         cand_t = load_list("cand_t", cand)
         n3_t = load_list("n3_t", n3)
         n4_t = load_list("n4_t", n4)
@@ -86,17 +86,17 @@ def tile_picked_pqcjgxbebz_none_po_kernel(
 
         def deal_words(dst, src):
             nc.vector.tensor_copy(
-                dst[:].bitcast(I32).rearrange("p (t c i) -> p c t i", t=PACK, i=4),
-                src[:].bitcast(I32).rearrange("p (c i t) -> p c t i", t=PACK, i=4),
+                dst[:].bitcast(I32).rearrange("p (u e c i) -> p c u i e", u=2, e=2, i=4),
+                src[:].bitcast(I32).rearrange("p (c i u e) -> p c u i e", u=2, e=2, i=4),
             )
 
         def deal_bytes(dst, src):
             nc.vector.tensor_copy(dst.rearrange("p (t m) -> p t m", t=PACK), src.rearrange("p (m t) -> p t m", t=PACK))
 
-        def place_scale_rows(plane):
+        def place_scale_rows(plane, queue):
             words = plane[:].bitcast(I32)
             for r in range(1, 4):
-                nc.sync.dma_start(words[r:P:32, :], words[8 * r : P : 32, :])
+                queue.dma_start(words[r:P:32, :], words[8 * r : P : 32, :])
 
         def product(banks, lhs_words, lhs_scales, rhs_words, rhs_scales):
             for t in range(PACK):
@@ -117,7 +117,7 @@ def tile_picked_pqcjgxbebz_none_po_kernel(
         plane1 = held.tile([P, H + S], U8, name="plane1", tag="bytes_a", align_bytes=64)
         deal_bytes(plane1[:, :H], got_b1[:, :H])
         nc.vector.tensor_copy(plane1[:, H:].bitcast(I32), got_b1[:, H:].bitcast(I32))
-        place_scale_rows(plane1)
+        place_scale_rows(plane1, nc.sync)
         got_k1 = held.tile([P, H], U32, name="got_k1", tag="words_a", align_bytes=64)
         nc.vector.tensor_copy(got_k1[:], d_tab[:].indirect(k1_t[:]))
         k1_w = held.tile([P, H], U32, name="k1_w", tag="words_b", align_bytes=64)
@@ -126,6 +126,9 @@ def tile_picked_pqcjgxbebz_none_po_kernel(
         nc.vector.tensor_copy(offs_w[:], x_tab[:].indirect(offs_t[:]))
         h_ps = [psum.tile([P, 2 * S], F32, name="h_ps%d" % t, tag="ha%d" % t) for t in range(PACK)]
         product(h_ps, k1_w, plane1, offs_w[:], plane1[:, H:])
+
+        got_b2 = held.tile([P, H], U8, name="got_b2", align_bytes=64)
+        nc.vector.tensor_copy(got_b2[:, :H], d_bytes[:].indirect(k2_t[:]))
 
         low = held.tile([P, PACK], F32, name="low")
         ea_bias = held.tile([P, PACK], F32, name="ea_bias")
@@ -140,16 +143,12 @@ def tile_picked_pqcjgxbebz_none_po_kernel(
             nc.scalar.activation(h_n2[:, t, :], h_win[t][:].indirect(n2_t[:]), ACT.Copy)
             nc.scalar.activation(gs_h[:, t, :], h_ps[t][:, :S], ACT.Copy, scale=gs_16[:, t : t + 1])
 
-        plane2 = held.tile([P, H + C + S], U8, name="plane2", align_bytes=64)
-        got_b2 = held.tile([P, H], U8, name="got_b2", align_bytes=64)
-        nc.vector.tensor_copy(got_b2[:], d_bytes[:].indirect(k2_t[:]))
-        deal_bytes(plane2[:, :H], got_b2[:])
-        got_b3 = held.tile([P, C + S], U8, name="got_b3", tag="bytes_a", align_bytes=64)
-        nc.vector.tensor_copy(got_b3[:, C:], x_bytes[:].indirect(two_t[:]))
-        nc.vector.tensor_copy(got_b3[:, :C], x_bytes[:].indirect(cand_t[:]))
-        deal_bytes(plane2[:, H : H + C], got_b3[:, :C])
-        nc.vector.tensor_copy(plane2[:, H + C :].bitcast(I32), got_b3[:, C:].bitcast(I32))
-        place_scale_rows(plane2)
+        got_two = held.tile([P, S], U8, name="got_two", tag="words_c", align_bytes=64)
+        nc.vector.tensor_copy(got_two[:], x_bytes[:].indirect(two_t[:]))
+        plane2 = held.tile([P, H + S], U8, name="plane2", align_bytes=64)
+        deal_bytes(plane2[:, :H], got_b2[:, :H])
+        nc.vector.tensor_copy(plane2[:, H:].bitcast(I32), got_two[:].bitcast(I32))
+        place_scale_rows(plane2, nc.sync)
         got_k2 = held.tile([P, H], U32, name="got_k2", tag="words_b", align_bytes=64)
         nc.vector.tensor_copy(got_k2[:], d_tab[:].indirect(k2_t[:]))
         k2_w = held.tile([P, H], U32, name="k2_w", tag="words_a", align_bytes=64)
@@ -157,13 +156,18 @@ def tile_picked_pqcjgxbebz_none_po_kernel(
         two_w = held.tile([P, S], U32, name="two_w", tag="words_c", align_bytes=64)
         nc.vector.tensor_copy(two_w[:], x_tab[:].indirect(two_t[:]))
         b_ps = [psum.tile([P, 2 * S], F32, name="b_ps%d" % t) for t in range(PACK)]
-        product(b_ps, k2_w, plane2, two_w[:], plane2[:, H + C :])
+        product(b_ps, k2_w, plane2, two_w[:], plane2[:, H:])
         for t in range(PACK):
             nc.scalar.activation(b_win[t][:, :S], b_ps[t][:, :S], ACT.Copy, scale=SIXTEENTH)
         for t in range(PACK):
             col = slice(t, t + 1)
             nc.scalar.activation(a_win[t][:, S:], b_win[t][:].indirect(n3_t[:]), ACT.Sigmoid, bias=sg_bias[:, col], scale=sl_t[:, col])
 
+        got_b3 = held.tile([P, C], U8, name="got_b3", tag="bytes_a", align_bytes=64)
+        nc.vector.tensor_copy(got_b3[:], x_bytes[:].indirect(cand_t[:]))
+        cand_s = held.tile([P, C], U8, name="cand_s", align_bytes=64)
+        deal_bytes(cand_s[:], got_b3[:])
+        place_scale_rows(cand_s, nc.sync)
         got_cand = held.tile([P, C], U32, name="got_cand", tag="words_b", align_bytes=64)
         nc.vector.tensor_copy(got_cand[:], x_tab[:].indirect(cand_t[:]))
         cand_w = held.tile([P, C], U32, name="cand_w", align_bytes=64)
@@ -173,16 +177,16 @@ def tile_picked_pqcjgxbebz_none_po_kernel(
             nc.vector.scalar_tensor_tensor(pull[:, t, :], b_win[t][:, S:], gs_m2[:, t : t + 1], h_n2[:, t, :], ALU.mult, ALU.mult)
         z_bf = held.tile([P, S * PACK], BF16, name="z_bf", align_bytes=64)
         nc.vector.tensor_tensor(
-            z_bf[:].rearrange("p (c i t) -> p c t i", i=4, t=PACK),
-            gs_h[:].rearrange("p t (c i) -> p c t i", i=4),
-            pull[:].rearrange("p t (c i) -> p c t i", i=4),
+            z_bf[:].rearrange("p (c i t) -> p c t i", i=2, t=PACK),
+            gs_h[:].rearrange("p t (c i) -> p c t i", i=2),
+            pull[:].rearrange("p t (c i) -> p c t i", i=2),
             ALU.add,
         )
         z_w = held.tile([P, S], U32, name="z_w", align_bytes=64)
         z_s = held.tile([P, S], U8, name="z_s", align_bytes=64)
         nc.vector.quantize_mx(out=z_w[:].bitcast(FP8X4), scales=z_s[:], in_=z_bf[:])
         a_ps = [psum.tile([P, 2 * S], F32, name="a_ps%d" % t, tag="ha%d" % t) for t in range(PACK)]
-        product(a_ps, cand_w, plane2[:, H : H + C], z_w[:], z_s[:])
+        product(a_ps, cand_w, cand_s, z_w[:], z_s[:])
 
         a_n4 = held.tile([P, PACK, S], F32, name="a_n4")
         gated = held.tile([P, PACK, S], F32, name="gated")
@@ -190,12 +194,18 @@ def tile_picked_pqcjgxbebz_none_po_kernel(
         out_rows = out_0.rearrange("(p t) j -> p t j", t=PACK)
         for t in range(PACK):
             nc.scalar.activation(a_win[t][:, :S], a_ps[t][:, :S], ACT.Copy, scale=-0.5 * SIXTEENTH)
-            nc.scalar.activation(a_n4[:, t, :], a_win[t][:].indirect(n4_t[:]), ACT.Copy)
             nc.vector.scalar_tensor_tensor(gated[:, t, :], a_win[t][:, :S], -2.0, a_win[t][:, S:], ALU.mult, ALU.mult)
-            nc.vector.tensor_tensor(y[:, t, :], gated[:, t, :], a_n4[:, t, :], ALU.add)
+            if t == 0:
+                nc.vector.tensor_tensor(y[:, t, :], a_win[t][:].indirect(n4_t[:]), gated[:, t, :], ALU.add)
+            else:
+                nc.scalar.activation(a_n4[:, t, :], a_win[t][:].indirect(n4_t[:]), ACT.Copy)
+                nc.vector.tensor_tensor(y[:, t, :], gated[:, t, :], a_n4[:, t, :], ALU.add)
             nc.sync.dma_start(out_rows[:, t, :], y[:, t, :])
         y_bf = held.tile([P, S * PACK], BF16, name="y_bf", align_bytes=64)
-        nc.vector.tensor_copy(y_bf[:].rearrange("p (c i t) -> p c t i", i=4, t=PACK), y[:].rearrange("p t (c i) -> p c t i", i=4))
+        woven = y_bf[:].rearrange("p (c i t) -> p c t i", i=2, t=PACK)
+        planes = y[:].rearrange("p t (c i) -> p c t i", i=2)
+        nc.vector.tensor_copy(woven[:, :80], planes[:, :80])
+        nc.scalar.copy(woven[:, 80:], planes[:, 80:])
         y_w = held.tile([P, S], U32, name="y_w", align_bytes=64)
         y_s = held.tile([P, S], U8, name="y_s", align_bytes=64)
         nc.vector.quantize_mx(out=y_w[:].bitcast(FP8X4), scales=y_s[:], in_=y_bf[:])

@@ -18,6 +18,7 @@ ACT = mybir.ActivationFunctionType
 P = 128
 PACK = 4
 SIXTEENTH = 0.0625
+VECTOR_TILES = 2
 
 
 def tile_picked_pqcjgxbebz_none_po_kernel(
@@ -54,13 +55,13 @@ def tile_picked_pqcjgxbebz_none_po_kernel(
         offs_t = load_list("offs_t", offs)
         x_bytes = load_scale_rows("x_bytes", x_scales, T)
         d_tab = load_words("d_tab", d_words, G)
-        x_tab = load_words("x_tab", x_words, T)
-        k2_t = load_list("k2_t", k2)
-        two_t = load_list("two_t", two)
         n1_t = load_list("n1_t", n1)
         n2_t = load_list("n2_t", n2)
-        cand_t = load_list("cand_t", cand)
         n3_t = load_list("n3_t", n3)
+        x_tab = load_words("x_tab", x_words, T)
+        two_t = load_list("two_t", two)
+        k2_t = load_list("k2_t", k2)
+        cand_t = load_list("cand_t", cand)
         n4_t = load_list("n4_t", n4)
         tau_t = load_rows("tau_t", tau)
         gs_t = load_rows("gs_t", gs)
@@ -120,15 +121,13 @@ def tile_picked_pqcjgxbebz_none_po_kernel(
         place_scale_rows(plane1, nc.sync)
         got_k1 = held.tile([P, H], U32, name="got_k1", tag="words_a", align_bytes=64)
         nc.vector.tensor_copy(got_k1[:], d_tab[:].indirect(k1_t[:]))
-        k1_w = held.tile([P, H], U32, name="k1_w", tag="words_b", align_bytes=64)
-        deal_words(k1_w, got_k1)
         offs_w = held.tile([P, S], U32, name="offs_w", tag="words_c", align_bytes=64)
         nc.vector.tensor_copy(offs_w[:], x_tab[:].indirect(offs_t[:]))
+        k1_w = held.tile([P, H], U32, name="k1_w", tag="words_b", align_bytes=64)
+        deal_words(k1_w, got_k1)
         h_ps = [psum.tile([P, 2 * S], F32, name="h_ps%d" % t, tag="ha%d" % t) for t in range(PACK)]
         product(h_ps, k1_w, plane1, offs_w[:], plane1[:, H:])
 
-        got_b2 = held.tile([P, H], U8, name="got_b2", align_bytes=64)
-        nc.vector.tensor_copy(got_b2[:, :H], d_bytes[:].indirect(k2_t[:]))
 
         low = held.tile([P, PACK], F32, name="low")
         ea_bias = held.tile([P, PACK], F32, name="ea_bias")
@@ -143,11 +142,13 @@ def tile_picked_pqcjgxbebz_none_po_kernel(
             nc.scalar.activation(h_n2[:, t, :], h_win[t][:].indirect(n2_t[:]), ACT.Copy)
             nc.scalar.activation(gs_h[:, t, :], h_ps[t][:, :S], ACT.Copy, scale=gs_16[:, t : t + 1])
 
-        got_two = held.tile([P, S], U8, name="got_two", tag="words_c", align_bytes=64)
+        got_two = held.tile([P, S], U8, name="got_two", tag="bytes_b", align_bytes=64)
         nc.vector.tensor_copy(got_two[:], x_bytes[:].indirect(two_t[:]))
-        plane2 = held.tile([P, H + S], U8, name="plane2", align_bytes=64)
-        deal_bytes(plane2[:, :H], got_b2[:, :H])
+        got_b2 = held.tile([P, H], U8, name="got_b2", tag="words_c", align_bytes=64)
+        nc.vector.tensor_copy(got_b2[:], d_bytes[:].indirect(k2_t[:]))
+        plane2 = held.tile([P, H + S], U8, name="plane2", tag="bytes_a", align_bytes=64)
         nc.vector.tensor_copy(plane2[:, H:].bitcast(I32), got_two[:].bitcast(I32))
+        deal_bytes(plane2[:, :H], got_b2[:])
         place_scale_rows(plane2, nc.sync)
         got_k2 = held.tile([P, H], U32, name="got_k2", tag="words_b", align_bytes=64)
         nc.vector.tensor_copy(got_k2[:], d_tab[:].indirect(k2_t[:]))
@@ -163,7 +164,7 @@ def tile_picked_pqcjgxbebz_none_po_kernel(
             col = slice(t, t + 1)
             nc.scalar.activation(a_win[t][:, S:], b_win[t][:].indirect(n3_t[:]), ACT.Sigmoid, bias=sg_bias[:, col], scale=sl_t[:, col])
 
-        got_b3 = held.tile([P, C], U8, name="got_b3", tag="bytes_a", align_bytes=64)
+        got_b3 = held.tile([P, C], U8, name="got_b3", tag="bytes_b", align_bytes=64)
         nc.vector.tensor_copy(got_b3[:], x_bytes[:].indirect(cand_t[:]))
         cand_s = held.tile([P, C], U8, name="cand_s", align_bytes=64)
         deal_bytes(cand_s[:], got_b3[:])
@@ -193,12 +194,14 @@ def tile_picked_pqcjgxbebz_none_po_kernel(
         y = held.tile([P, PACK, S], F32, name="y")
         out_rows = out_0.rearrange("(p t) j -> p t j", t=PACK)
         for t in range(PACK):
-            nc.scalar.activation(a_win[t][:, :S], a_ps[t][:, :S], ACT.Copy, scale=-0.5 * SIXTEENTH)
-            nc.vector.scalar_tensor_tensor(gated[:, t, :], a_win[t][:, :S], -2.0, a_win[t][:, S:], ALU.mult, ALU.mult)
-            if t == 0:
+            if t < VECTOR_TILES:
+                nc.vector.tensor_scalar(a_win[t][:, :S], a_ps[t][:, :S], -0.5 * SIXTEENTH, None, ALU.mult)
+                nc.vector.scalar_tensor_tensor(gated[:, t, :], a_ps[t][:, :S], SIXTEENTH, a_win[t][:, S:], ALU.mult, ALU.mult)
                 nc.vector.tensor_tensor(y[:, t, :], a_win[t][:].indirect(n4_t[:]), gated[:, t, :], ALU.add)
             else:
+                nc.scalar.activation(a_win[t][:, :S], a_ps[t][:, :S], ACT.Copy, scale=-0.5 * SIXTEENTH)
                 nc.scalar.activation(a_n4[:, t, :], a_win[t][:].indirect(n4_t[:]), ACT.Copy)
+                nc.vector.scalar_tensor_tensor(gated[:, t, :], a_win[t][:, :S], -2.0, a_win[t][:, S:], ALU.mult, ALU.mult)
                 nc.vector.tensor_tensor(y[:, t, :], gated[:, t, :], a_n4[:, t, :], ALU.add)
             nc.sync.dma_start(out_rows[:, t, :], y[:, t, :])
         y_bf = held.tile([P, S * PACK], BF16, name="y_bf", align_bytes=64)

@@ -3,7 +3,7 @@ from contextlib import ExitStack
 import concourse.mybir as mybir
 
 K, T, S, G, H, C = 512, 1024, 256, 2048, 512, 512
-FLOPS = 3 * 2 * K * H * S
+FLOPS = 2 * K * S * (H + H + C)
 
 F32 = mybir.dt.float32
 BF16 = mybir.dt.bfloat16
@@ -17,8 +17,11 @@ ACT = mybir.ActivationFunctionType
 
 P = 128
 PACK = 4
+BLOCKS = 16
+QUADRANT = 32
 SIXTEENTH = 0.0625
 VECTOR_TILES = 2
+VECTOR_PAIRS = 80
 
 
 def tile_picked_pqcjgxbebz_none_po_kernel(
@@ -36,7 +39,7 @@ def tile_picked_pqcjgxbebz_none_po_kernel(
 
         def load_scale_rows(name, src, width):
             tile = held.tile([P, width], U8, name=name, align_bytes=64)
-            rows = src[0].bitcast(I32).unsqueeze(1).to_broadcast([16, 8, width // 4])
+            rows = src[0].bitcast(I32).unsqueeze(1).to_broadcast([BLOCKS, P // BLOCKS, width // 4])
             nc.sync.dma_start(tile[:].bitcast(I32), rows)
             return tile
 
@@ -45,7 +48,7 @@ def tile_picked_pqcjgxbebz_none_po_kernel(
             nc.sync.dma_start(tile[:].bitcast(I32), src[0].rearrange("p n t -> p (n t)").bitcast(I32))
             return tile
 
-        def load_rows(name, src):
+        def load_row_values(name, src):
             tile = held.tile([P, PACK], F32, name=name)
             nc.gpsimd.dma_start(tile[:], src.rearrange("(p t) o -> p (t o)", t=PACK))
             return tile
@@ -63,10 +66,10 @@ def tile_picked_pqcjgxbebz_none_po_kernel(
         k2_t = load_list("k2_t", k2)
         cand_t = load_list("cand_t", cand)
         n4_t = load_list("n4_t", n4)
-        tau_t = load_rows("tau_t", tau)
-        gs_t = load_rows("gs_t", gs)
-        sl_t = load_rows("sl_t", sl)
-        th_t = load_rows("th_t", th)
+        tau_t = load_row_values("tau_t", tau)
+        gs_t = load_row_values("gs_t", gs)
+        sl_t = load_row_values("sl_t", sl)
+        th_t = load_row_values("th_t", th)
 
         neg_tau = held.tile([P, PACK], F32, name="neg_tau")
         nc.gpsimd.tensor_scalar(neg_tau[:], tau_t[:], -1.0, 0.0, ALU.mult, ALU.add)
@@ -82,6 +85,8 @@ def tile_picked_pqcjgxbebz_none_po_kernel(
         h_win = [held.tile([P, 2 * S], F32, name="h_win%d" % t) for t in range(PACK)]
         b_win = [held.tile([P, 2 * S], F32, name="b_win%d" % t) for t in range(PACK)]
         a_win = [held.tile([P, 2 * S], F32, name="a_win%d" % t) for t in range(PACK)]
+        ea = [b_win[t][:, S:] for t in range(PACK)]
+        sg = [a_win[t][:, S:] for t in range(PACK)]
         for t in range(PACK):
             nc.vector.memset(h_win[t][:, S:], 0.0)
 
@@ -94,10 +99,10 @@ def tile_picked_pqcjgxbebz_none_po_kernel(
         def deal_bytes(dst, src):
             nc.vector.tensor_copy(dst.rearrange("p (t m) -> p t m", t=PACK), src.rearrange("p (m t) -> p t m", t=PACK))
 
-        def place_scale_rows(plane, queue):
-            words = plane[:].bitcast(I32)
+        def place_scale_rows(scales):
+            view = scales[:].bitcast(I32)
             for r in range(1, 4):
-                queue.dma_start(words[r:P:32, :], words[8 * r : P : 32, :])
+                nc.sync.dma_start(view[r:P:QUADRANT, :], view[8 * r : P : QUADRANT, :])
 
         def product(banks, lhs_words, lhs_scales, rhs_words, rhs_scales):
             for t in range(PACK):
@@ -112,22 +117,28 @@ def tile_picked_pqcjgxbebz_none_po_kernel(
                     stop=True,
                 )
 
-        got_b1 = held.tile([P, H + S], U8, name="got_b1", align_bytes=64)
-        nc.vector.tensor_copy(got_b1[:, :H], d_bytes[:].indirect(k1_t[:]))
-        nc.vector.tensor_copy(got_b1[:, H:], x_bytes[:].indirect(offs_t[:]))
-        plane1 = held.tile([P, H + S], U8, name="plane1", tag="bytes_a", align_bytes=64)
-        deal_bytes(plane1[:, :H], got_b1[:, :H])
-        nc.vector.tensor_copy(plane1[:, H:].bitcast(I32), got_b1[:, H:].bitcast(I32))
-        place_scale_rows(plane1, nc.sync)
-        got_k1 = held.tile([P, H], U32, name="got_k1", tag="words_a", align_bytes=64)
-        nc.vector.tensor_copy(got_k1[:], d_tab[:].indirect(k1_t[:]))
-        offs_w = held.tile([P, S], U32, name="offs_w", tag="words_c", align_bytes=64)
+        def woven(tile):
+            return tile[:].rearrange("p (c i t) -> p c t i", i=2, t=PACK)
+
+        def in_pairs(tile):
+            return tile[:].rearrange("p t (c i) -> p c t i", i=2)
+
+
+        h_bytes = held.tile([P, H + S], U8, name="h_bytes", align_bytes=64)
+        nc.vector.tensor_copy(h_bytes[:, :H], d_bytes[:].indirect(k1_t[:]))
+        nc.vector.tensor_copy(h_bytes[:, H:], x_bytes[:].indirect(offs_t[:]))
+        h_scales = held.tile([P, H + S], U8, name="h_scales", tag="scales", align_bytes=64)
+        deal_bytes(h_scales[:, :H], h_bytes[:, :H])
+        nc.vector.tensor_copy(h_scales[:, H:].bitcast(I32), h_bytes[:, H:].bitcast(I32))
+        place_scale_rows(h_scales)
+        k1_got = held.tile([P, H], U32, name="k1_got", tag="words_a", align_bytes=64)
+        nc.vector.tensor_copy(k1_got[:], d_tab[:].indirect(k1_t[:]))
+        offs_w = held.tile([P, S], U32, name="offs_w", tag="moving", align_bytes=64)
         nc.vector.tensor_copy(offs_w[:], x_tab[:].indirect(offs_t[:]))
         k1_w = held.tile([P, H], U32, name="k1_w", tag="words_b", align_bytes=64)
-        deal_words(k1_w, got_k1)
-        h_ps = [psum.tile([P, 2 * S], F32, name="h_ps%d" % t, tag="ha%d" % t) for t in range(PACK)]
-        product(h_ps, k1_w, plane1, offs_w[:], plane1[:, H:])
-
+        deal_words(k1_w, k1_got)
+        h_ps = [psum.tile([P, 2 * S], F32, name="h_ps%d" % t, tag="h_then_a%d" % t) for t in range(PACK)]
+        product(h_ps, k1_w, h_scales, offs_w[:], h_scales[:, H:])
 
         low = held.tile([P, PACK], F32, name="low")
         ea_bias = held.tile([P, PACK], F32, name="ea_bias")
@@ -137,58 +148,57 @@ def tile_picked_pqcjgxbebz_none_po_kernel(
             col = slice(t, t + 1)
             nc.vector.tensor_scalar(h_win[t][:, :S], h_ps[t][:, :S], SIXTEENTH, None, ALU.mult, ALU.min, accum_out=low[:, col])
             nc.gpsimd.tensor_tensor(ea_bias[:, col], tau_t[:, col], low[:, col], ALU.mult)
-            nc.scalar.activation(b_win[t][:, S:], h_win[t][:].indirect(n1_t[:]), ACT.Exp, bias=ea_bias[:, col], scale=neg_tau[:, col])
+            nc.scalar.activation(ea[t], h_win[t][:].indirect(n1_t[:]), ACT.Exp, bias=ea_bias[:, col], scale=neg_tau[:, col])
         for t in range(PACK):
             nc.scalar.activation(h_n2[:, t, :], h_win[t][:].indirect(n2_t[:]), ACT.Copy)
             nc.scalar.activation(gs_h[:, t, :], h_ps[t][:, :S], ACT.Copy, scale=gs_16[:, t : t + 1])
 
-        got_two = held.tile([P, S], U8, name="got_two", tag="bytes_b", align_bytes=64)
-        nc.vector.tensor_copy(got_two[:], x_bytes[:].indirect(two_t[:]))
-        got_b2 = held.tile([P, H], U8, name="got_b2", tag="words_c", align_bytes=64)
-        nc.vector.tensor_copy(got_b2[:], d_bytes[:].indirect(k2_t[:]))
-        plane2 = held.tile([P, H + S], U8, name="plane2", tag="bytes_a", align_bytes=64)
-        nc.vector.tensor_copy(plane2[:, H:].bitcast(I32), got_two[:].bitcast(I32))
-        deal_bytes(plane2[:, :H], got_b2[:])
-        place_scale_rows(plane2, nc.sync)
-        got_k2 = held.tile([P, H], U32, name="got_k2", tag="words_b", align_bytes=64)
-        nc.vector.tensor_copy(got_k2[:], d_tab[:].indirect(k2_t[:]))
-        k2_w = held.tile([P, H], U32, name="k2_w", tag="words_a", align_bytes=64)
-        deal_words(k2_w, got_k2)
-        two_w = held.tile([P, S], U32, name="two_w", tag="words_c", align_bytes=64)
+        two_bytes = held.tile([P, S], U8, name="two_bytes", tag="x_gathered", align_bytes=64)
+        nc.vector.tensor_copy(two_bytes[:], x_bytes[:].indirect(two_t[:]))
+        k2_bytes = held.tile([P, H], U8, name="k2_bytes", tag="moving", align_bytes=64)
+        nc.vector.tensor_copy(k2_bytes[:], d_bytes[:].indirect(k2_t[:]))
+        b_scales = held.tile([P, H + S], U8, name="b_scales", tag="scales", align_bytes=64)
+        nc.vector.tensor_copy(b_scales[:, H:].bitcast(I32), two_bytes[:].bitcast(I32))
+        deal_bytes(b_scales[:, :H], k2_bytes[:])
+        place_scale_rows(b_scales)
+        k2_got = held.tile([P, H], U32, name="k2_got", tag="words_b", align_bytes=64)
+        nc.vector.tensor_copy(k2_got[:], d_tab[:].indirect(k2_t[:]))
+        two_w = held.tile([P, S], U32, name="two_w", tag="moving", align_bytes=64)
         nc.vector.tensor_copy(two_w[:], x_tab[:].indirect(two_t[:]))
+        k2_w = held.tile([P, H], U32, name="k2_w", tag="words_a", align_bytes=64)
+        deal_words(k2_w, k2_got)
         b_ps = [psum.tile([P, 2 * S], F32, name="b_ps%d" % t) for t in range(PACK)]
-        product(b_ps, k2_w, plane2, two_w[:], plane2[:, H:])
+        product(b_ps, k2_w, b_scales, two_w[:], b_scales[:, H:])
         for t in range(PACK):
             nc.scalar.activation(b_win[t][:, :S], b_ps[t][:, :S], ACT.Copy, scale=SIXTEENTH)
         for t in range(PACK):
             col = slice(t, t + 1)
-            nc.scalar.activation(a_win[t][:, S:], b_win[t][:].indirect(n3_t[:]), ACT.Sigmoid, bias=sg_bias[:, col], scale=sl_t[:, col])
+            nc.scalar.activation(sg[t], b_win[t][:].indirect(n3_t[:]), ACT.Sigmoid, bias=sg_bias[:, col], scale=sl_t[:, col])
 
-        got_b3 = held.tile([P, C], U8, name="got_b3", tag="bytes_b", align_bytes=64)
-        nc.vector.tensor_copy(got_b3[:], x_bytes[:].indirect(cand_t[:]))
-        cand_s = held.tile([P, C], U8, name="cand_s", align_bytes=64)
-        deal_bytes(cand_s[:], got_b3[:])
-        place_scale_rows(cand_s, nc.sync)
-        got_cand = held.tile([P, C], U32, name="got_cand", tag="words_b", align_bytes=64)
-        nc.vector.tensor_copy(got_cand[:], x_tab[:].indirect(cand_t[:]))
-        cand_w = held.tile([P, C], U32, name="cand_w", align_bytes=64)
-        deal_words(cand_w, got_cand)
+        cand_bytes = held.tile([P, C], U8, name="cand_bytes", tag="x_gathered", align_bytes=64)
+        nc.vector.tensor_copy(cand_bytes[:].rearrange("p (t m) -> p m t", t=PACK), x_bytes[:].indirect(cand_t[:]))
+        cand_w = held.tile([P, C], U32, name="cand_w", tag="words_b", align_bytes=64)
+        nc.vector.tensor_copy(cand_w[:].rearrange("p (t m) -> p m t", t=PACK), x_tab[:].indirect(cand_t[:]))
+        cand_scales = held.tile([P, C], U8, name="cand_scales", align_bytes=64)
+        nc.vector.tensor_copy(cand_scales[:].bitcast(I32), cand_bytes[:].bitcast(I32))
+        place_scale_rows(cand_scales)
+
         pull = held.tile([P, PACK, S], F32, name="pull")
         for t in range(PACK):
-            nc.vector.scalar_tensor_tensor(pull[:, t, :], b_win[t][:, S:], gs_m2[:, t : t + 1], h_n2[:, t, :], ALU.mult, ALU.mult)
+            nc.vector.scalar_tensor_tensor(pull[:, t, :], ea[t], gs_m2[:, t : t + 1], h_n2[:, t, :], ALU.mult, ALU.mult)
         z_bf = held.tile([P, S * PACK], BF16, name="z_bf", align_bytes=64)
-        nc.vector.tensor_tensor(
-            z_bf[:].rearrange("p (c i t) -> p c t i", i=2, t=PACK),
-            gs_h[:].rearrange("p t (c i) -> p c t i", i=2),
-            pull[:].rearrange("p t (c i) -> p c t i", i=2),
-            ALU.add,
-        )
         z_w = held.tile([P, S], U32, name="z_w", align_bytes=64)
-        z_s = held.tile([P, S], U8, name="z_s", align_bytes=64)
-        nc.vector.quantize_mx(out=z_w[:].bitcast(FP8X4), scales=z_s[:], in_=z_bf[:])
-        a_ps = [psum.tile([P, 2 * S], F32, name="a_ps%d" % t, tag="ha%d" % t) for t in range(PACK)]
-        product(a_ps, cand_w, cand_s, z_w[:], z_s[:])
+        z_scales = held.tile([P, S], U8, name="z_scales", align_bytes=64)
+        for half in range(2):
+            pairs = slice(half * S // 4, (half + 1) * S // 4)
+            nc.vector.tensor_tensor(woven(z_bf)[:, pairs], in_pairs(gs_h)[:, pairs], in_pairs(pull)[:, pairs], ALU.add)
+        for half in range(2):
+            cols = slice(half * S // 2, (half + 1) * S // 2)
+            values = slice(PACK * cols.start, PACK * cols.stop)
+            nc.vector.quantize_mx(out=z_w[:, cols].bitcast(FP8X4), scales=z_scales[:, cols], in_=z_bf[:, values])
 
+        a_ps = [psum.tile([P, 2 * S], F32, name="a_ps%d" % t, tag="h_then_a%d" % t) for t in range(PACK)]
+        product(a_ps, cand_w, cand_scales, z_w[:], z_scales[:])
         a_n4 = held.tile([P, PACK, S], F32, name="a_n4")
         gated = held.tile([P, PACK, S], F32, name="gated")
         y = held.tile([P, PACK, S], F32, name="y")
@@ -196,23 +206,22 @@ def tile_picked_pqcjgxbebz_none_po_kernel(
         for t in range(PACK):
             if t < VECTOR_TILES:
                 nc.vector.tensor_scalar(a_win[t][:, :S], a_ps[t][:, :S], -0.5 * SIXTEENTH, None, ALU.mult)
-                nc.vector.scalar_tensor_tensor(gated[:, t, :], a_ps[t][:, :S], SIXTEENTH, a_win[t][:, S:], ALU.mult, ALU.mult)
+                nc.vector.scalar_tensor_tensor(gated[:, t, :], a_ps[t][:, :S], SIXTEENTH, sg[t], ALU.mult, ALU.mult)
                 nc.vector.tensor_tensor(y[:, t, :], a_win[t][:].indirect(n4_t[:]), gated[:, t, :], ALU.add)
             else:
                 nc.scalar.activation(a_win[t][:, :S], a_ps[t][:, :S], ACT.Copy, scale=-0.5 * SIXTEENTH)
                 nc.scalar.activation(a_n4[:, t, :], a_win[t][:].indirect(n4_t[:]), ACT.Copy)
-                nc.vector.scalar_tensor_tensor(gated[:, t, :], a_win[t][:, :S], -2.0, a_win[t][:, S:], ALU.mult, ALU.mult)
+                nc.vector.scalar_tensor_tensor(gated[:, t, :], a_win[t][:, :S], -2.0, sg[t], ALU.mult, ALU.mult)
                 nc.vector.tensor_tensor(y[:, t, :], gated[:, t, :], a_n4[:, t, :], ALU.add)
             nc.sync.dma_start(out_rows[:, t, :], y[:, t, :])
+
         y_bf = held.tile([P, S * PACK], BF16, name="y_bf", align_bytes=64)
-        woven = y_bf[:].rearrange("p (c i t) -> p c t i", i=2, t=PACK)
-        planes = y[:].rearrange("p t (c i) -> p c t i", i=2)
-        nc.vector.tensor_copy(woven[:, :80], planes[:, :80])
-        nc.scalar.copy(woven[:, 80:], planes[:, 80:])
+        nc.vector.tensor_copy(woven(y_bf)[:, :VECTOR_PAIRS], in_pairs(y)[:, :VECTOR_PAIRS])
+        nc.scalar.copy(woven(y_bf)[:, VECTOR_PAIRS:], in_pairs(y)[:, VECTOR_PAIRS:])
         y_w = held.tile([P, S], U32, name="y_w", align_bytes=64)
-        y_s = held.tile([P, S], U8, name="y_s", align_bytes=64)
-        nc.vector.quantize_mx(out=y_w[:].bitcast(FP8X4), scales=y_s[:], in_=y_bf[:])
+        y_scales = held.tile([P, S], U8, name="y_scales", align_bytes=64)
+        nc.vector.quantize_mx(out=y_w[:].bitcast(FP8X4), scales=y_scales[:], in_=y_bf[:])
         nc.sync.dma_start(out_1[0].rearrange("p c r -> p (c r)").bitcast(I32), y_w[:].bitcast(I32))
         for r in range(4):
             queue = nc.scalar if r % 2 else nc.sync
-            queue.dma_start(out_2[0].bitcast(I32)[r:16:4, :], y_s[:].bitcast(I32)[r:P:32, :])
+            queue.dma_start(out_2[0].bitcast(I32)[r:BLOCKS:4, :], y_scales[:].bitcast(I32)[r:P:QUADRANT, :])

from contextlib import ExitStack

import concourse.mybir as mybir

K, T, S, G, H, C = 512, 1024, 256, 2048, 512, 512
FLOPS = 2 * K * S * (H + H + C)

F32 = mybir.dt.float32
BF16 = mybir.dt.bfloat16
I32 = mybir.dt.int32
U32 = mybir.dt.uint32
U16 = mybir.dt.uint16
U8 = mybir.dt.uint8
FP8X4 = mybir.dt.float8_e4m3fn_x4
ALU = mybir.AluOpType
ACT = mybir.ActivationFunctionType

P = 128
PACK = 4
BLOCKS = 16
QUADRANT = 32
SIXTEENTH = 0.0625
VECTOR_TILES = 2
VECTOR_PAIRS = 80


def tile_picked_pqcjgxbebz_none_po_kernel(
    tc, x_words, x_scales, d_words, d_scales, tau, gs, sl, th, offs, k1, n1, n2, cand, two, k2, n3, n4, out_0, out_1, out_2
):
    nc = tc.nc
    with ExitStack() as ctx:
        held = ctx.enter_context(tc.tile_pool(name="held", bufs=1))
        psum = ctx.enter_context(tc.psum_pool(name="psum", bufs=1))

        def load_list(name, src):
            tile = held.tile(list(src.shape), U16, name=name)
            nc.sync.dma_start(tile[:], src)
            return tile

        def load_scale_rows(name, src, width):
            tile = held.tile([P, width], U8, name=name, align_bytes=64)
            rows = src[0].bitcast(I32).unsqueeze(1).to_broadcast([BLOCKS, P // BLOCKS, width // 4])
            nc.sync.dma_start(tile[:].bitcast(I32), rows)
            return tile

        def load_words(name, src, width):
            tile = held.tile([P, width], U32, name=name, align_bytes=64)
            nc.sync.dma_start(tile[:].bitcast(I32), src[0].rearrange("p n t -> p (n t)").bitcast(I32))
            return tile

        def load_row_values(name, src):
            tile = held.tile([P, PACK], F32, name=name)
            nc.gpsimd.dma_start(tile[:], src.rearrange("(p t) o -> p (t o)", t=PACK))
            return tile

        k1_t = load_list("k1_t", k1)
        d_bytes = load_scale_rows("d_bytes", d_scales, G)
        offs_t = load_list("offs_t", offs)
        x_bytes = load_scale_rows("x_bytes", x_scales, T)
        d_tab = load_words("d_tab", d_words, G)
        n1_t = load_list("n1_t", n1)
        n2_t = load_list("n2_t", n2)
        n3_t = load_list("n3_t", n3)
        x_tab = load_words("x_tab", x_words, T)
        two_t = load_list("two_t", two)
        k2_t = load_list("k2_t", k2)
        cand_t = load_list("cand_t", cand)
        n4_t = load_list("n4_t", n4)
        tau_t = load_row_values("tau_t", tau)
        gs_t = load_row_values("gs_t", gs)
        sl_t = load_row_values("sl_t", sl)
        th_t = load_row_values("th_t", th)

        neg_tau = held.tile([P, PACK], F32, name="neg_tau")
        nc.gpsimd.tensor_scalar(neg_tau[:], tau_t[:], -1.0, 0.0, ALU.mult, ALU.add)
        gs_m2 = held.tile([P, PACK], F32, name="gs_m2")
        nc.gpsimd.tensor_scalar(gs_m2[:], gs_t[:], -2.0, 0.0, ALU.mult, ALU.add)
        gs_16 = held.tile([P, PACK], F32, name="gs_16")
        nc.gpsimd.tensor_scalar(gs_16[:], gs_t[:], SIXTEENTH, 0.0, ALU.mult, ALU.add)
        sl_th = held.tile([P, PACK], F32, name="sl_th")
        nc.gpsimd.tensor_tensor(sl_th[:], sl_t[:], th_t[:], ALU.mult)
        sg_bias = held.tile([P, PACK], F32, name="sg_bias")
        nc.gpsimd.tensor_scalar(sg_bias[:], sl_th[:], -1.0, 0.0, ALU.mult, ALU.add)

        h_win = [held.tile([P, 2 * S], F32, name="h_win%d" % t) for t in range(PACK)]
        b_win = [held.tile([P, 2 * S], F32, name="b_win%d" % t) for t in range(PACK)]
        a_win = [held.tile([P, 2 * S], F32, name="a_win%d" % t) for t in range(PACK)]
        ea = [b_win[t][:, S:] for t in range(PACK)]
        sg = [a_win[t][:, S:] for t in range(PACK)]
        for t in range(PACK):
            nc.vector.memset(h_win[t][:, S:], 0.0)

        def deal_words(dst, src):
            nc.vector.tensor_copy(
                dst[:].bitcast(I32).rearrange("p (u e c i) -> p c u i e", u=2, e=2, i=4),
                src[:].bitcast(I32).rearrange("p (c i u e) -> p c u i e", u=2, e=2, i=4),
            )

        def deal_bytes(dst, src):
            nc.vector.tensor_copy(dst.rearrange("p (t m) -> p t m", t=PACK), src.rearrange("p (m t) -> p t m", t=PACK))

        def place_scale_rows(scales):
            view = scales[:].bitcast(I32)
            for r in range(1, 4):
                nc.sync.dma_start(view[r:P:QUADRANT, :], view[8 * r : P : QUADRANT, :])

        def product(banks, lhs_words, lhs_scales, rhs_words, rhs_scales):
            for t in range(PACK):
                cols = slice(t * P, (t + 1) * P)
                nc.tensor.matmul_mx(
                    out=banks[t][:, :S],
                    lhsT=lhs_words[:, cols].bitcast(FP8X4),
                    lhsT_scale=lhs_scales[:, cols],
                    rhs=rhs_words.bitcast(FP8X4),
                    rhs_scale=rhs_scales,
                    start=True,
                    stop=True,
                )

        def woven(tile):
            return tile[:].rearrange("p (c i t) -> p c t i", i=2, t=PACK)

        def in_pairs(tile):
            return tile[:].rearrange("p t (c i) -> p c t i", i=2)


        h_bytes = held.tile([P, H + S], U8, name="h_bytes", align_bytes=64)
        nc.vector.tensor_copy(h_bytes[:, :H], d_bytes[:].indirect(k1_t[:]))
        nc.vector.tensor_copy(h_bytes[:, H:], x_bytes[:].indirect(offs_t[:]))
        h_scales = held.tile([P, H + S], U8, name="h_scales", tag="scales", align_bytes=64)
        deal_bytes(h_scales[:, :H], h_bytes[:, :H])
        nc.vector.tensor_copy(h_scales[:, H:].bitcast(I32), h_bytes[:, H:].bitcast(I32))
        place_scale_rows(h_scales)
        k1_got = held.tile([P, H], U32, name="k1_got", tag="words_a", align_bytes=64)
        nc.vector.tensor_copy(k1_got[:], d_tab[:].indirect(k1_t[:]))
        offs_w = held.tile([P, S], U32, name="offs_w", tag="moving", align_bytes=64)
        nc.vector.tensor_copy(offs_w[:], x_tab[:].indirect(offs_t[:]))
        k1_w = held.tile([P, H], U32, name="k1_w", tag="words_b", align_bytes=64)
        deal_words(k1_w, k1_got)
        h_ps = [psum.tile([P, 2 * S], F32, name="h_ps%d" % t, tag="h_then_a%d" % t) for t in range(PACK)]
        product(h_ps, k1_w, h_scales, offs_w[:], h_scales[:, H:])

        low = held.tile([P, PACK], F32, name="low")
        ea_bias = held.tile([P, PACK], F32, name="ea_bias")
        h_n2 = held.tile([P, PACK, S], F32, name="h_n2")
        gs_h = held.tile([P, PACK, S], F32, name="gs_h")
        for t in range(PACK):
            col = slice(t, t + 1)
            nc.vector.tensor_scalar(h_win[t][:, :S], h_ps[t][:, :S], SIXTEENTH, None, ALU.mult, ALU.min, accum_out=low[:, col])
            nc.gpsimd.tensor_tensor(ea_bias[:, col], tau_t[:, col], low[:, col], ALU.mult)
            nc.scalar.activation(ea[t], h_win[t][:].indirect(n1_t[:]), ACT.Exp, bias=ea_bias[:, col], scale=neg_tau[:, col])
        for t in range(PACK):
            nc.scalar.activation(h_n2[:, t, :], h_win[t][:].indirect(n2_t[:]), ACT.Copy)
            nc.scalar.activation(gs_h[:, t, :], h_ps[t][:, :S], ACT.Copy, scale=gs_16[:, t : t + 1])

        two_bytes = held.tile([P, S], U8, name="two_bytes", tag="x_gathered", align_bytes=64)
        nc.vector.tensor_copy(two_bytes[:], x_bytes[:].indirect(two_t[:]))
        k2_bytes = held.tile([P, H], U8, name="k2_bytes", tag="moving", align_bytes=64)
        nc.vector.tensor_copy(k2_bytes[:], d_bytes[:].indirect(k2_t[:]))
        b_scales = held.tile([P, H + S], U8, name="b_scales", tag="scales", align_bytes=64)
        nc.vector.tensor_copy(b_scales[:, H:].bitcast(I32), two_bytes[:].bitcast(I32))
        deal_bytes(b_scales[:, :H], k2_bytes[:])
        place_scale_rows(b_scales)
        k2_got = held.tile([P, H], U32, name="k2_got", tag="words_b", align_bytes=64)
        nc.vector.tensor_copy(k2_got[:], d_tab[:].indirect(k2_t[:]))
        two_w = held.tile([P, S], U32, name="two_w", tag="moving", align_bytes=64)
        nc.vector.tensor_copy(two_w[:], x_tab[:].indirect(two_t[:]))
        k2_w = held.tile([P, H], U32, name="k2_w", tag="words_a", align_bytes=64)
        deal_words(k2_w, k2_got)
        b_ps = [psum.tile([P, 2 * S], F32, name="b_ps%d" % t) for t in range(PACK)]
        product(b_ps, k2_w, b_scales, two_w[:], b_scales[:, H:])
        for t in range(PACK):
            nc.scalar.activation(b_win[t][:, :S], b_ps[t][:, :S], ACT.Copy, scale=SIXTEENTH)
        for t in range(PACK):
            col = slice(t, t + 1)
            nc.scalar.activation(sg[t], b_win[t][:].indirect(n3_t[:]), ACT.Sigmoid, bias=sg_bias[:, col], scale=sl_t[:, col])

        cand_bytes = held.tile([P, C], U8, name="cand_bytes", tag="x_gathered", align_bytes=64)
        nc.vector.tensor_copy(cand_bytes[:].rearrange("p (t m) -> p m t", t=PACK), x_bytes[:].indirect(cand_t[:]))
        cand_w = held.tile([P, C], U32, name="cand_w", tag="words_b", align_bytes=64)
        nc.vector.tensor_copy(cand_w[:].rearrange("p (t m) -> p m t", t=PACK), x_tab[:].indirect(cand_t[:]))
        cand_scales = held.tile([P, C], U8, name="cand_scales", align_bytes=64)
        nc.vector.tensor_copy(cand_scales[:].bitcast(I32), cand_bytes[:].bitcast(I32))
        place_scale_rows(cand_scales)

        pull = held.tile([P, PACK, S], F32, name="pull")
        for t in range(PACK):
            nc.vector.scalar_tensor_tensor(pull[:, t, :], ea[t], gs_m2[:, t : t + 1], h_n2[:, t, :], ALU.mult, ALU.mult)
        z_bf = held.tile([P, S * PACK], BF16, name="z_bf", align_bytes=64)
        z_w = held.tile([P, S], U32, name="z_w", align_bytes=64)
        z_scales = held.tile([P, S], U8, name="z_scales", align_bytes=64)
        for half in range(2):
            pairs = slice(half * S // 4, (half + 1) * S // 4)
            nc.vector.tensor_tensor(woven(z_bf)[:, pairs], in_pairs(gs_h)[:, pairs], in_pairs(pull)[:, pairs], ALU.add)
        for half in range(2):
            cols = slice(half * S // 2, (half + 1) * S // 2)
            values = slice(PACK * cols.start, PACK * cols.stop)
            nc.vector.quantize_mx(out=z_w[:, cols].bitcast(FP8X4), scales=z_scales[:, cols], in_=z_bf[:, values])

        a_ps = [psum.tile([P, 2 * S], F32, name="a_ps%d" % t, tag="h_then_a%d" % t) for t in range(PACK)]
        product(a_ps, cand_w, cand_scales, z_w[:], z_scales[:])
        a_n4 = held.tile([P, PACK, S], F32, name="a_n4")
        gated = held.tile([P, PACK, S], F32, name="gated")
        y = held.tile([P, PACK, S], F32, name="y")
        out_rows = out_0.rearrange("(p t) j -> p t j", t=PACK)
        for t in range(PACK):
            if t < VECTOR_TILES:
                nc.vector.tensor_scalar(a_win[t][:, :S], a_ps[t][:, :S], -0.5 * SIXTEENTH, None, ALU.mult)
                nc.vector.scalar_tensor_tensor(gated[:, t, :], a_ps[t][:, :S], SIXTEENTH, sg[t], ALU.mult, ALU.mult)
                nc.vector.tensor_tensor(y[:, t, :], a_win[t][:].indirect(n4_t[:]), gated[:, t, :], ALU.add)
            else:
                nc.scalar.activation(a_win[t][:, :S], a_ps[t][:, :S], ACT.Copy, scale=-0.5 * SIXTEENTH)
                nc.scalar.activation(a_n4[:, t, :], a_win[t][:].indirect(n4_t[:]), ACT.Copy)
                nc.vector.scalar_tensor_tensor(gated[:, t, :], a_win[t][:, :S], -2.0, sg[t], ALU.mult, ALU.mult)
                nc.vector.tensor_tensor(y[:, t, :], gated[:, t, :], a_n4[:, t, :], ALU.add)
            nc.sync.dma_start(out_rows[:, t, :], y[:, t, :])

        y_bf = held.tile([P, S * PACK], BF16, name="y_bf", align_bytes=64)
        nc.vector.tensor_copy(woven(y_bf)[:, :VECTOR_PAIRS], in_pairs(y)[:, :VECTOR_PAIRS])
        nc.scalar.copy(woven(y_bf)[:, VECTOR_PAIRS:], in_pairs(y)[:, VECTOR_PAIRS:])
        y_w = held.tile([P, S], U32, name="y_w", align_bytes=64)
        y_scales = held.tile([P, S], U8, name="y_scales", align_bytes=64)
        nc.vector.quantize_mx(out=y_w[:].bitcast(FP8X4), scales=y_scales[:], in_=y_bf[:])
        nc.sync.dma_start(out_1[0].rearrange("p c r -> p (c r)").bitcast(I32), y_w[:].bitcast(I32))
        for r in range(4):
            queue = nc.scalar if r % 2 else nc.sync
            queue.dma_start(out_2[0].bitcast(I32)[r:BLOCKS:4, :], y_scales[:].bitcast(I32)[r:P:QUADRANT, :])
